import numpy as np
import ml_dtypes


def mxq(x, axis, fmt="e4m3"):
    dtype, down = {"e4m3": (ml_dtypes.float8_e4m3fn, 7), "e5m2": (ml_dtypes.float8_e5m2, 14)}[fmt]
    v = np.moveaxis(np.asarray(x, np.float32).astype(ml_dtypes.bfloat16).astype(np.float64), axis, -1)
    blocks = v.reshape(v.shape[:-1] + (-1, 32))
    amax = np.abs(blocks).max(-1, keepdims=True)
    byte = np.maximum(np.where(amax > 0, np.frexp(amax)[1] - 1 + 127, 0) - down, 1)
    scale = np.exp2(byte - 127.0)
    codes = (blocks / scale).astype(np.float32).astype(dtype).astype(np.float64)
    return np.moveaxis((codes * scale).reshape(v.shape), -1, axis)


WIDE = False


def mx_kscale(k):
    if not WIDE:
        return np.ones(k)
    levels = np.array([10, -10, 5, -5, 0])
    if k % 512:
        return np.exp2(np.random.permutation(np.resize(levels, k // 32))).repeat(32)
    a = np.empty((k // 512, 16))
    for p in range(k // 512):
        a[p, :8] = np.random.permutation(np.resize(levels, 8))
        for g in range(8):
            far = levels[np.abs(levels - a[p, g]) >= 10]
            a[p, g + 8] = far[np.random.randint(len(far))]
    return np.exp2(a.ravel()).repeat(32)


def f64(x):
    return np.asarray(x).astype(np.float64)


def striped(idx):
    return np.tile(idx.reshape(-1, 16).T, (8, 1)).astype(np.uint16)


def unstriped(offs):
    return offs[:16].T.reshape(-1).astype(np.int64)


def gelu(v):
    return 0.5 * v * (1.0 + np.tanh(np.sqrt(2.0 / np.pi) * (v + 0.044715 * v**3)))


K, T, D, S, V, N = 512, 1024, 4, 1024, 256, 512


def setup_inputs():
    n = np.random.standard_normal
    s = mx_kscale(K)[:, None]
    return {
        "xT": (n((K, T)) * s).astype(np.float32),
        "w": (n((D, K, N)) / np.sqrt(D * K) / s[None]).astype(np.float32),
        "b": (0.3 * n((N, 1))).astype(np.float32),
        "gate": np.tile(np.random.uniform(0.2, 1.0, S), (N, 1)).astype(np.float32),
        "offs": striped(np.random.permutation(T)[:S]),
    }


def reference(xT, w, b, gate, offs):
    idx = unstriped(offs)
    xq = mxq(f64(xT)[:, idx], 0, "e4m3")
    wq = mxq(f64(w), 1, "e4m3")
    y = sum(wq[d].T @ xq[:, d * V:(d + 1) * V] for d in range(D))
    y = gelu(y + f64(b))
    out = np.zeros((N, T))
    out[:, idx] = f64(gate) * np.tile(y, (1, D))
    return out

@@ -1,0 +1,146 @@
+from contextlib import ExitStack
+
+import concourse.mybir as mybir
+
+F32 = mybir.dt.float32
+BF16 = mybir.dt.bfloat16
+U32 = mybir.dt.uint32
+U16 = mybir.dt.uint16
+U8 = mybir.dt.uint8
+FP8X4 = mybir.dt.float8_e4m3fn_x4
+MULT = mybir.AluOpType.mult
+GELU = mybir.ActivationFunctionType.Gelu_apprx_tanh
+
+P = 128
+K, T, D, V, N = 512, 1024, 4, 256, 512
+BLOCKS = N // P
+FLOPS = 2 * D * K * N * V
+
+TOKEN_CHUNKS = ((0, 512), (512, 256), (768, 256))
+
+
+def interleave(copy, grouped, raw):
+    copy(
+        grouped.rearrange("p (c i) j -> p c j i", i=4),
+        raw.rearrange("p j (c i) -> p c j i", i=4),
+    )
+
+
+def tile_picked_tome_lin_gelu_sub_e_kernel(tc, xT, w, b, gate, offs, out):
+    nc = tc.nc
+    with ExitStack() as ctx:
+        keep = ctx.enter_context(tc.tile_pool(name="keep", bufs=1))
+        psum = ctx.enter_context(tc.psum_pool(name="psum", bufs=1))
+
+        warm = keep.tile([P, 1], F32, name="warm")
+        nc.vector.memset(warm[:], 0.0)
+        nc.scalar.activation(warm[:], warm[:], GELU)
+
+        x_words = keep.tile([P, T], U32, name="x_words", align_bytes=64)
+        x_bytes = keep.tile([P, T], U8, name="x_bytes", align_bytes=64)
+        nc.gpsimd.memset(x_bytes[:], 0)
+        g_words = keep.tile([P, T], U32, name="g_words", align_bytes=64)
+        g_bytes = keep.tile([P, T], U8, name="g_bytes", align_bytes=64)
+
+        offsets = keep.tile([P, T // 16], U16, name="offsets")
+        x_raw = []
+        for i, (t0, n) in enumerate(TOKEN_CHUNKS):
+            raw = keep.tile([P, 4, n], F32, name="x_raw%d" % i)
+            nc.sync.dma_start(raw[:], xT[:, t0 : t0 + n].rearrange("(p j) t -> p j t", j=4))
+            x_raw.append(raw)
+            if i == 0:
+                nc.sync.dma_start(offsets[:], offs)
+
+        w_raw = {}
+
+        def load_w(block, count):
+            for d in range(D):
+                raw = keep.tile([P, 4, count * P], F32, name="w_raw%d_%d" % (block, d))
+                cols = slice(block * P, (block + count) * P)
+                nc.sync.dma_start(raw[:], w[d, :, cols].rearrange("(p j) m -> p j m", j=4))
+                for c in range(count):
+                    w_raw[block + c, d] = raw[:, :, c * P : (c + 1) * P]
+
+        gates = [keep.tile([P, T], F32, name="gate%d" % m) for m in range(BLOCKS)]
+
+        def load_gate(m):
+            nc.sync.dma_start(gates[m][:], gate[m * P : (m + 1) * P, :])
+
+        bias = keep.tile([P, BLOCKS], F32, name="bias")
+        load_w(0, 1)
+        nc.sync.dma_start(bias[:], b.rearrange("(m p) o -> p (m o)", p=P))
+        load_gate(0)
+        load_w(1, 1)
+        load_gate(1)
+        load_w(2, 2)
+        load_gate(2)
+        load_gate(3)
+
+        for i, (t0, n) in enumerate(TOKEN_CHUNKS):
+            grouped = keep.tile([P, n, 4], BF16, name="x_grouped%d" % i, align_bytes=64)
+            h = n // 2
+            interleave(nc.vector.tensor_copy, grouped[:, 0:h, :], x_raw[i][:, :, 0:h])
+            interleave(nc.scalar.copy, grouped[:, h:n, :], x_raw[i][:, :, h:n])
+            nc.vector.quantize_mx(
+                out=x_words[:, t0 : t0 + n].bitcast(FP8X4),
+                scales=x_bytes[:, t0 : t0 + n],
+                in_=grouped[:].rearrange("p t j -> p (t j)"),
+            )
+
+        w_words, w_bytes = [], []
+
+        def prepare_w(m):
+            grouped = keep.tile([P, D * P, 4], BF16, name="w_grouped%d" % m, align_bytes=64)
+            for d in range(D):
+                interleave(nc.scalar.copy, grouped[:, d * P : (d + 1) * P, :], w_raw[m, d])
+            words = keep.tile([P, D * P], U32, name="w_words%d" % m, align_bytes=64)
+            scales = keep.tile([P, D * P], U8, name="w_bytes%d" % m, align_bytes=64)
+            nc.vector.quantize_mx(
+                out=words[:].bitcast(FP8X4), scales=scales[:], in_=grouped[:].rearrange("p c j -> p (c j)")
+            )
+            w_words.append(words)
+            w_bytes.append(scales)
+
+        def product(m):
+            acc = psum.tile([P, V], F32, name="acc%d" % m)
+            for d in range(D):
+                nc.tensor.matmul_mx(
+                    out=acc[:],
+                    lhsT=w_words[m][:, d * P : (d + 1) * P].bitcast(FP8X4),
+                    lhsT_scale=w_bytes[m][:, d * P : (d + 1) * P],
+                    rhs=g_words[:, d * V : (d + 1) * V].bitcast(FP8X4),
+                    rhs_scale=g_bytes[:, d * V : (d + 1) * V],
+                    start=(d == 0),
+                    stop=(d == D - 1),
+                )
+            y = keep.tile([P, 2, V], F32, name="y%d" % m)
+            for r in range(2):
+                nc.scalar.activation(y[:, r, :], acc[:], GELU, bias=bias[:, m : m + 1])
+            return y
+
+        for h in range(2):
+            entries = slice(h * 512, (h + 1) * 512)
+            columns = slice(h * 32, (h + 1) * 32)
+            nc.vector.tensor_copy(g_words[:, entries], x_words[:].indirect(offsets[:, columns]))
+            nc.vector.tensor_copy(g_bytes[:, entries], x_bytes[:].indirect(offsets[:, columns]))
+
+        windows = [keep.tile([P, T], F32, name="window%d" % m) for m in range(BLOCKS)]
+
+        def scatter(m, y, h):
+            nc.vector.tensor_tensor(
+                windows[m][:].indirect(offsets[:, h * 32 : (h + 1) * 32]),
+                y[:].rearrange("p r v -> p (r v)"),
+                gates[m][:, h * 512 : (h + 1) * 512],
+                MULT,
+            )
+
+        for pair in range(2):
+            ms = (2 * pair, 2 * pair + 1)
+            ys = {}
+            for m in ms:
+                prepare_w(m)
+                ys[m] = product(m)
+                scatter(m, ys[m], 0)
+            for m in ms:
+                scatter(m, ys[m], 1)
+                nc.sync.dma_start(out[m * P : (m + 1) * P, :], windows[m][:])

@@ -1,6 +1,7 @@
 from contextlib import ExitStack
 
 import concourse.mybir as mybir
+from concourse.masks import make_identity
 
 F32 = mybir.dt.float32
 BF16 = mybir.dt.bfloat16
@@ -14,9 +15,11 @@ GELU = mybir.ActivationFunctionType.Gelu_apprx_tanh
 P = 128
 K, T, D, V, N = 512, 1024, 4, 256, 512
 BLOCKS = N // P
+M = 256
+H = V // 2
 FLOPS = 2 * D * K * N * V
 
-TOKEN_CHUNKS = ((0, 512), (512, 256), (768, 256))
+TOKEN_CHUNKS = ((0, 256, 160), (256, 256, 160), (512, 256, 160), (768, 256, 192))
 
 
 def interleave(copy, grouped, raw):
@@ -32,6 +35,15 @@ def tile_picked_tome_lin_gelu_sub_e_kernel(tc, xT, w, b, gate, offs, out):
         keep = ctx.enter_context(tc.tile_pool(name="keep", bufs=1))
         psum = ctx.enter_context(tc.psum_pool(name="psum", bufs=1))
 
+        bias = keep.tile([P, BLOCKS], F32, name="bias")
+        bias_rows = keep.tile([P, P], F32, name="bias_rows")
+        nc.gpsimd.memset(bias_rows[:], 0.0)
+        nc.scalar.dma_start(bias_rows[0:BLOCKS, :], b.rearrange("(m p) o -> m (p o)", p=P))
+        identity = keep.tile([P, P], F32, name="identity")
+        make_identity(nc, identity[:])
+        bias_columns = psum.tile([P, P], F32, name="bias_columns", tag="acc31")
+        nc.tensor.transpose(bias_columns[:], bias_rows[:], identity[:])
+        nc.scalar.copy(bias[:], bias_columns[:, 0:BLOCKS])
         warm = keep.tile([P, 1], F32, name="warm")
         nc.vector.memset(warm[:], 0.0)
         nc.scalar.activation(warm[:], warm[:], GELU)
@@ -39,46 +51,38 @@ def tile_picked_tome_lin_gelu_sub_e_kernel(tc, xT, w, b, gate, offs, out):
         x_words = keep.tile([P, T], U32, name="x_words", align_bytes=64)
         x_bytes = keep.tile([P, T], U8, name="x_bytes", align_bytes=64)
         nc.gpsimd.memset(x_bytes[:], 0)
-        g_words = keep.tile([P, T], U32, name="g_words", align_bytes=64)
-        g_bytes = keep.tile([P, T], U8, name="g_bytes", align_bytes=64)
 
         offsets = keep.tile([P, T // 16], U16, name="offsets")
         x_raw = []
-        for i, (t0, n) in enumerate(TOKEN_CHUNKS):
+        for i, (t0, n, h) in enumerate(TOKEN_CHUNKS):
             raw = keep.tile([P, 4, n], F32, name="x_raw%d" % i)
             nc.sync.dma_start(raw[:], xT[:, t0 : t0 + n].rearrange("(p j) t -> p j t", j=4))
             x_raw.append(raw)
             if i == 0:
                 nc.sync.dma_start(offsets[:], offs)
 
-        w_raw = {}
-
-        def load_w(block, count):
-            for d in range(D):
-                raw = keep.tile([P, 4, count * P], F32, name="w_raw%d_%d" % (block, d))
-                cols = slice(block * P, (block + count) * P)
-                nc.sync.dma_start(raw[:], w[d, :, cols].rearrange("(p j) m -> p j m", j=4))
-                for c in range(count):
-                    w_raw[block + c, d] = raw[:, :, c * P : (c + 1) * P]
-
+        w_raw = [[keep.tile([P, 4, 2 * M], F32, name="w_raw%d%d" % (q, h), tag="w_raw%d%d" % (q, h)) for h in range(2)] for q in range(2)]
         gates = [keep.tile([P, T], F32, name="gate%d" % m) for m in range(BLOCKS)]
+
+        def load_w(q):
+            for d in range(D):
+                nc.sync.dma_start(
+                    w_raw[q][d // 2][:, :, d % 2 * M : (d % 2 + 1) * M],
+                    w[d, :, q * M : (q + 1) * M].rearrange("(p j) m -> p j m", j=4),
+                )
 
         def load_gate(m):
             nc.sync.dma_start(gates[m][:], gate[m * P : (m + 1) * P, :])
 
-        bias = keep.tile([P, BLOCKS], F32, name="bias")
-        load_w(0, 1)
-        nc.sync.dma_start(bias[:], b.rearrange("(m p) o -> p (m o)", p=P))
+        load_w(0)
         load_gate(0)
-        load_w(1, 1)
         load_gate(1)
-        load_w(2, 2)
+        load_w(1)
         load_gate(2)
         load_gate(3)
 
-        for i, (t0, n) in enumerate(TOKEN_CHUNKS):
+        for i, (t0, n, h) in enumerate(TOKEN_CHUNKS):
             grouped = keep.tile([P, n, 4], BF16, name="x_grouped%d" % i, align_bytes=64)
-            h = n // 2
             interleave(nc.vector.tensor_copy, grouped[:, 0:h, :], x_raw[i][:, :, 0:h])
             interleave(nc.scalar.copy, grouped[:, h:n, :], x_raw[i][:, :, h:n])
             nc.vector.quantize_mx(
@@ -87,60 +91,86 @@ def tile_picked_tome_lin_gelu_sub_e_kernel(tc, xT, w, b, gate, offs, out):
                 in_=grouped[:].rearrange("p t j -> p (t j)"),
             )
 
-        w_words, w_bytes = [], []
+        w_words = {}
 
-        def prepare_w(m):
-            grouped = keep.tile([P, D * P, 4], BF16, name="w_grouped%d" % m, align_bytes=64)
-            for d in range(D):
-                interleave(nc.scalar.copy, grouped[:, d * P : (d + 1) * P, :], w_raw[m, d])
-            words = keep.tile([P, D * P], U32, name="w_words%d" % m, align_bytes=64)
-            scales = keep.tile([P, D * P], U8, name="w_bytes%d" % m, align_bytes=64)
+        def prepare_w(name, q, h, c0, c1, step):
+            width = c1 - c0
+            grouped = keep.tile([P, width, 4], BF16, name="w_grouped" + name, tag="w_grouped" + name, align_bytes=64)
+            for c in range(0, width, step):
+                interleave(nc.scalar.copy, grouped[:, c : c + step, :], w_raw[q][h][:, :, c0 + c : c0 + c + step])
+            words = keep.tile([P, width], U32, name="w_words" + name, align_bytes=64)
+            scales = keep.tile([P, width], U8, name="w_bytes" + name, align_bytes=64)
             nc.vector.quantize_mx(
                 out=words[:].bitcast(FP8X4), scales=scales[:], in_=grouped[:].rearrange("p c j -> p (c j)")
             )
-            w_words.append(words)
-            w_bytes.append(scales)
+            for c in range(0, width, P):
+                d, r = divmod(c0 + c, M)
+                w_words[2 * q + r // P, 2 * h + d] = (words[:, c : c + P].bitcast(FP8X4), scales[:, c : c + P])
+
+        def gather(words, scales, e0, e1):
+            columns = slice(e0 // 16, e1 // 16)
+            nc.vector.tensor_copy(words, x_words[:].indirect(offsets[:, columns]))
+            nc.vector.tensor_copy(scales, x_bytes[:].indirect(offsets[:, columns]))
+
+        accs = [[psum.tile([P, H], F32, name="acc%d%d" % (m, h), tag="acc%d%d" % (m, h)) for h in range(2)] for m in range(BLOCKS)]
 
         def product(m):
-            acc = psum.tile([P, V], F32, name="acc%d" % m)
-            for d in range(D):
-                nc.tensor.matmul_mx(
-                    out=acc[:],
-                    lhsT=w_words[m][:, d * P : (d + 1) * P].bitcast(FP8X4),
-                    lhsT_scale=w_bytes[m][:, d * P : (d + 1) * P],
-                    rhs=g_words[:, d * V : (d + 1) * V].bitcast(FP8X4),
-                    rhs_scale=g_bytes[:, d * V : (d + 1) * V],
-                    start=(d == 0),
-                    stop=(d == D - 1),
-                )
-            y = keep.tile([P, 2, V], F32, name="y%d" % m)
-            for r in range(2):
-                nc.scalar.activation(y[:, r, :], acc[:], GELU, bias=bias[:, m : m + 1])
-            return y
-
-        for h in range(2):
-            entries = slice(h * 512, (h + 1) * 512)
-            columns = slice(h * 32, (h + 1) * 32)
-            nc.vector.tensor_copy(g_words[:, entries], x_words[:].indirect(offsets[:, columns]))
-            nc.vector.tensor_copy(g_bytes[:, entries], x_bytes[:].indirect(offsets[:, columns]))
+            for h in range(2):
+                for d in range(D):
+                    lhs, lhs_scale = w_words[m, d]
+                    if d < 3:
+                        c0 = d * V + h * H
+                        rhs, rhs_scale = words012[:, c0 : c0 + H], bytes012[:, c0 : c0 + H]
+                    else:
+                        rhs, rhs_scale = words3[h][:], bytes3[h][:]
+                    nc.tensor.matmul_mx(
+                        out=accs[m][h][:],
+                        lhsT=lhs,
+                        lhsT_scale=lhs_scale,
+                        rhs=rhs.bitcast(FP8X4),
+                        rhs_scale=rhs_scale,
+                        start=(d == 0),
+                        stop=(d == D - 1),
+                    )
 
         windows = [keep.tile([P, T], F32, name="window%d" % m) for m in range(BLOCKS)]
 
-        def scatter(m, y, h):
+        def put_back(m, e0, e1, tag):
+            y = keep.tile([P, e1 - e0], F32, name="y" + tag, tag=tag)
+            for e in range(e0, e1, H):
+                nc.scalar.activation(y[:, e - e0 : e - e0 + H], accs[m][e // H % 2][:], GELU, bias=bias[:, m : m + 1])
             nc.vector.tensor_tensor(
-                windows[m][:].indirect(offsets[:, h * 32 : (h + 1) * 32]),
-                y[:].rearrange("p r v -> p (r v)"),
-                gates[m][:, h * 512 : (h + 1) * 512],
-                MULT,
+                windows[m][:].indirect(offsets[:, e0 // 16 : e1 // 16]), y[:], gates[m][:, e0:e1], MULT
             )
-
-        for pair in range(2):
-            ms = (2 * pair, 2 * pair + 1)
-            ys = {}
-            for m in ms:
-                prepare_w(m)
-                ys[m] = product(m)
-                scatter(m, ys[m], 0)
-            for m in ms:
-                scatter(m, ys[m], 1)
+            if e1 == T:
                 nc.sync.dma_start(out[m * P : (m + 1) * P, :], windows[m][:])
+
+        words012 = keep.tile([P, 3 * V], U32, name="words012", align_bytes=64)
+        bytes012 = keep.tile([P, 3 * V], U8, name="bytes012", align_bytes=64)
+        words3 = [keep.tile([P, H], U32, name="words3a", align_bytes=64)]
+        bytes3 = [keep.tile([P, H], U8, name="bytes3a", align_bytes=64)]
+        gather(words012[:], bytes012[:], 0, 3 * V)
+        gather(words3[0][:], bytes3[0][:], 3 * V, 3 * V + H)
+        prepare_w("0_d01", 0, 0, 0, 2 * M, M)
+        prepare_w("0_d2", 0, 1, 0, M, M)
+        prepare_w("0_d3a", 0, 1, M, M + P, P)
+        prepare_w("0_d3b", 0, 1, M + P, 2 * M, P)
+        words3.append(keep.tile([P, H], U32, name="words3b", tag="w_grouped0_d3a", align_bytes=64))
+        bytes3.append(keep.tile([P, H], U8, name="bytes3b", tag="w_grouped0_d3b", align_bytes=64))
+        gather(words3[1][:], bytes3[1][:], 3 * V + H, 4 * V)
+
+        product(0)
+        product(1)
+        put_back(0, 0, 128, "y0a")
+        put_back(1, 0, 256, "y1a")
+        put_back(0, 128, 640, "y0b")
+        put_back(1, 256, 768, "y1b")
+        prepare_w("1_d01", 1, 0, 0, 2 * M, M)
+        put_back(0, 640, 1024, "w_raw10")
+        prepare_w("1_d23", 1, 1, 0, 2 * M, M)
+        put_back(1, 768, 1024, "w_raw11")
+        product(2)
+        product(3)
+        for e in (0, 512):
+            for m in (2, 3):
+                put_back(m, e, e + 512, "y%d_%d" % (m, e))

@@ -14,12 +14,14 @@ GELU = mybir.ActivationFunctionType.Gelu_apprx_tanh
 
 P = 128
 K, T, D, V, N = 512, 1024, 4, 256, 512
+PACK = K // P
 BLOCKS = N // P
-M = 256
-H = V // 2
+HALF = 2 * P
+OFFSETS = 16
 FLOPS = 2 * D * K * N * V
 
-TOKEN_CHUNKS = ((0, 256, 160), (256, 256, 160), (512, 256, 160), (768, 256, 192))
+TOKEN_CHUNKS = ((0, 384, 256), (384, 384, 256), (768, 256, 176))
+QUANTISE_TOKENS = 256
 
 
 def interleave(copy, grouped, raw):
@@ -29,21 +31,31 @@ def interleave(copy, grouped, raw):
     )
 
 
+def quantise(nc, words, scales, grouped):
+    nc.vector.quantize_mx(out=words.bitcast(FP8X4), scales=scales, in_=grouped.rearrange("p c j -> p (c j)"))
+
+
 def tile_picked_tome_lin_gelu_sub_e_kernel(tc, xT, w, b, gate, offs, out):
     nc = tc.nc
     with ExitStack() as ctx:
         keep = ctx.enter_context(tc.tile_pool(name="keep", bufs=1))
         psum = ctx.enter_context(tc.psum_pool(name="psum", bufs=1))
 
-        bias = keep.tile([P, BLOCKS], F32, name="bias")
         bias_rows = keep.tile([P, P], F32, name="bias_rows")
         nc.gpsimd.memset(bias_rows[:], 0.0)
         nc.scalar.dma_start(bias_rows[0:BLOCKS, :], b.rearrange("(m p) o -> m (p o)", p=P))
         identity = keep.tile([P, P], F32, name="identity")
         make_identity(nc, identity[:])
-        bias_columns = psum.tile([P, P], F32, name="bias_columns", tag="acc31")
+        bias_columns = psum.tile([P, P], F32, name="bias_columns")
         nc.tensor.transpose(bias_columns[:], bias_rows[:], identity[:])
+        bias = keep.tile([P, BLOCKS], F32, name="bias")
         nc.scalar.copy(bias[:], bias_columns[:, 0:BLOCKS])
+        bias_block1 = []
+        for h in range(2):
+            column = keep.tile([P, 1], F32, name="bias_block1_%d" % h, tag="w_grouped_C%d" % h, align_bytes=64)
+            nc.scalar.copy(column[:], bias_columns[:, 1:2])
+            bias_block1.append(column)
+
         warm = keep.tile([P, 1], F32, name="warm")
         nc.vector.memset(warm[:], 0.0)
         nc.scalar.activation(warm[:], warm[:], GELU)
@@ -52,125 +64,129 @@ def tile_picked_tome_lin_gelu_sub_e_kernel(tc, xT, w, b, gate, offs, out):
         x_bytes = keep.tile([P, T], U8, name="x_bytes", align_bytes=64)
         nc.gpsimd.memset(x_bytes[:], 0)
 
-        offsets = keep.tile([P, T // 16], U16, name="offsets")
+        offsets = keep.tile([P, T // OFFSETS], U16, name="offsets")
         x_raw = []
-        for i, (t0, n, h) in enumerate(TOKEN_CHUNKS):
-            raw = keep.tile([P, 4, n], F32, name="x_raw%d" % i)
-            nc.sync.dma_start(raw[:], xT[:, t0 : t0 + n].rearrange("(p j) t -> p j t", j=4))
+        for i, (t0, n, _) in enumerate(TOKEN_CHUNKS):
+            raw = keep.tile([P, PACK, n], F32, name="x_raw%d" % i)
+            nc.sync.dma_start(raw[:], xT[:, t0 : t0 + n].rearrange("(p j) t -> p j t", j=PACK))
             x_raw.append(raw)
-            if i == 0:
+            if i == 1:
                 nc.sync.dma_start(offsets[:], offs)
 
-        w_raw = [[keep.tile([P, 4, 2 * M], F32, name="w_raw%d%d" % (q, h), tag="w_raw%d%d" % (q, h)) for h in range(2)] for q in range(2)]
+        w_raw = [
+            [keep.tile([P, PACK, 2 * HALF], F32, name="w_raw%d%d" % (q, h), tag="w_raw%d%d" % (q, h)) for h in range(2)]
+            for q in range(2)
+        ]
         gates = [keep.tile([P, T], F32, name="gate%d" % m) for m in range(BLOCKS)]
-
-        def load_w(q):
+        for q in range(2):
             for d in range(D):
                 nc.sync.dma_start(
-                    w_raw[q][d // 2][:, :, d % 2 * M : (d % 2 + 1) * M],
-                    w[d, :, q * M : (q + 1) * M].rearrange("(p j) m -> p j m", j=4),
+                    w_raw[q][d // 2][:, :, d % 2 * HALF : (d % 2 + 1) * HALF],
+                    w[d, :, q * HALF : (q + 1) * HALF].rearrange("(p j) r -> p j r", j=PACK),
                 )
-
-        def load_gate(m):
-            nc.sync.dma_start(gates[m][:], gate[m * P : (m + 1) * P, :])
-
-        load_w(0)
-        load_gate(0)
-        load_gate(1)
-        load_w(1)
-        load_gate(2)
-        load_gate(3)
+            for m in (2 * q, 2 * q + 1):
+                nc.sync.dma_start(gates[m][:], gate[m * P : (m + 1) * P, :])
 
         for i, (t0, n, h) in enumerate(TOKEN_CHUNKS):
-            grouped = keep.tile([P, n, 4], BF16, name="x_grouped%d" % i, align_bytes=64)
+            grouped = keep.tile([P, n, PACK], BF16, name="x_grouped%d" % i, align_bytes=64)
             interleave(nc.vector.tensor_copy, grouped[:, 0:h, :], x_raw[i][:, :, 0:h])
             interleave(nc.scalar.copy, grouped[:, h:n, :], x_raw[i][:, :, h:n])
-            nc.vector.quantize_mx(
-                out=x_words[:, t0 : t0 + n].bitcast(FP8X4),
-                scales=x_bytes[:, t0 : t0 + n],
-                in_=grouped[:].rearrange("p t j -> p (t j)"),
-            )
+            for q0 in range(0, n, QUANTISE_TOKENS):
+                q1 = min(n, q0 + QUANTISE_TOKENS)
+                tokens = slice(t0 + q0, t0 + q1)
+                quantise(nc, x_words[:, tokens], x_bytes[:, tokens], grouped[:, q0:q1, :])
 
-        w_words = {}
+        w_codes = {}
 
-        def prepare_w(name, q, h, c0, c1, step):
-            width = c1 - c0
-            grouped = keep.tile([P, width, 4], BF16, name="w_grouped" + name, tag="w_grouped" + name, align_bytes=64)
-            for c in range(0, width, step):
-                interleave(nc.scalar.copy, grouped[:, c : c + step, :], w_raw[q][h][:, :, c0 + c : c0 + c + step])
-            words = keep.tile([P, width], U32, name="w_words" + name, align_bytes=64)
-            scales = keep.tile([P, width], U8, name="w_bytes" + name, align_bytes=64)
-            nc.vector.quantize_mx(
-                out=words[:].bitcast(FP8X4), scales=scales[:], in_=grouped[:].rearrange("p c j -> p (c j)")
-            )
-            for c in range(0, width, P):
-                d, r = divmod(c0 + c, M)
-                w_words[2 * q + r // P, 2 * h + d] = (words[:, c : c + P].bitcast(FP8X4), scales[:, c : c + P])
+        def prepare_w(name, q, rows, places):
+            count = len(rows)
+            width = count * len(places)
+            grouped = keep.tile([P, width, PACK], BF16, name="w_grouped_" + name, tag="w_grouped_" + name, align_bytes=64)
+            words = keep.tile([P, width], U32, name="w_words_" + name, align_bytes=64)
+            scales = keep.tile([P, width], U8, name="w_bytes_" + name, align_bytes=64)
+            for i, d in enumerate(places):
+                c0 = d % 2 * HALF + rows[0]
+                interleave(
+                    nc.scalar.copy,
+                    grouped[:, i * count : (i + 1) * count, :],
+                    w_raw[q][d // 2][:, :, c0 : c0 + count],
+                )
+                for r in range(0, count, P):
+                    cols = slice(i * count + r, i * count + r + P)
+                    w_codes[(q * HALF + rows[0] + r) // P, d] = (words[:, cols], scales[:, cols])
+            quantise(nc, words[:], scales[:], grouped[:])
 
-        def gather(words, scales, e0, e1):
-            columns = slice(e0 // 16, e1 // 16)
-            nc.vector.tensor_copy(words, x_words[:].indirect(offsets[:, columns]))
-            nc.vector.tensor_copy(scales, x_bytes[:].indirect(offsets[:, columns]))
-
-        accs = [[psum.tile([P, H], F32, name="acc%d%d" % (m, h), tag="acc%d%d" % (m, h)) for h in range(2)] for m in range(BLOCKS)]
+        accs = [psum.tile([P, V], F32, name="acc%d" % m) for m in range(BLOCKS)]
+        windows = [keep.tile([P, T], F32, name="window%d" % m) for m in range(BLOCKS)]
+        g_words, g_bytes = [], []
 
         def product(m):
-            for h in range(2):
-                for d in range(D):
-                    lhs, lhs_scale = w_words[m, d]
-                    if d < 3:
-                        c0 = d * V + h * H
-                        rhs, rhs_scale = words012[:, c0 : c0 + H], bytes012[:, c0 : c0 + H]
-                    else:
-                        rhs, rhs_scale = words3[h][:], bytes3[h][:]
-                    nc.tensor.matmul_mx(
-                        out=accs[m][h][:],
-                        lhsT=lhs,
-                        lhsT_scale=lhs_scale,
-                        rhs=rhs.bitcast(FP8X4),
-                        rhs_scale=rhs_scale,
-                        start=(d == 0),
-                        stop=(d == D - 1),
-                    )
+            for d in range(D):
+                words, scales = w_codes[m, d]
+                piece = slice(d % 2 * V, (d % 2 + 1) * V)
+                nc.tensor.matmul_mx(
+                    out=accs[m][:],
+                    lhsT=words.bitcast(FP8X4),
+                    lhsT_scale=scales,
+                    rhs=g_words[d // 2][:, piece].bitcast(FP8X4),
+                    rhs_scale=g_bytes[d // 2][:, piece],
+                    start=(d == 0),
+                    stop=(d == D - 1),
+                )
 
-        windows = [keep.tile([P, T], F32, name="window%d" % m) for m in range(BLOCKS)]
+        def activate(m, columns, name, tag):
+            y = keep.tile([P, len(columns) * V], F32, name=name, tag=tag)
+            for r, column in enumerate(columns):
+                nc.scalar.activation(y[:, r * V : (r + 1) * V], accs[m][:], GELU, bias=column)
+            return y
 
-        def put_back(m, e0, e1, tag):
-            y = keep.tile([P, e1 - e0], F32, name="y" + tag, tag=tag)
-            for e in range(e0, e1, H):
-                nc.scalar.activation(y[:, e - e0 : e - e0 + H], accs[m][e // H % 2][:], GELU, bias=bias[:, m : m + 1])
+        def scatter(m, y, d0, count):
+            entries = slice(d0 * V, (d0 + count) * V)
             nc.vector.tensor_tensor(
-                windows[m][:].indirect(offsets[:, e0 // 16 : e1 // 16]), y[:], gates[m][:, e0:e1], MULT
+                windows[m][:].indirect(offsets[:, d0 * V // OFFSETS : (d0 + count) * V // OFFSETS]),
+                y[:, 0 : count * V],
+                gates[m][:, entries],
+                MULT,
             )
-            if e1 == T:
+            if d0 + count == D:
                 nc.sync.dma_start(out[m * P : (m + 1) * P, :], windows[m][:])
 
-        words012 = keep.tile([P, 3 * V], U32, name="words012", align_bytes=64)
-        bytes012 = keep.tile([P, 3 * V], U8, name="bytes012", align_bytes=64)
-        words3 = [keep.tile([P, H], U32, name="words3a", align_bytes=64)]
-        bytes3 = [keep.tile([P, H], U8, name="bytes3a", align_bytes=64)]
-        gather(words012[:], bytes012[:], 0, 3 * V)
-        gather(words3[0][:], bytes3[0][:], 3 * V, 3 * V + H)
-        prepare_w("0_d01", 0, 0, 0, 2 * M, M)
-        prepare_w("0_d2", 0, 1, 0, M, M)
-        prepare_w("0_d3a", 0, 1, M, M + P, P)
-        prepare_w("0_d3b", 0, 1, M + P, 2 * M, P)
-        words3.append(keep.tile([P, H], U32, name="words3b", tag="w_grouped0_d3a", align_bytes=64))
-        bytes3.append(keep.tile([P, H], U8, name="bytes3b", tag="w_grouped0_d3b", align_bytes=64))
-        gather(words3[1][:], bytes3[1][:], 3 * V + H, 4 * V)
+        def bias_of(m):
+            return bias[:, m : m + 1]
+
+        block0, block1, both_blocks = range(0, P), range(P, HALF), range(0, HALF)
+
+        for h in range(2):
+            columns = slice(h * 2 * V // OFFSETS, (h + 1) * 2 * V // OFFSETS)
+            words = keep.tile([P, 2 * V], U32, name="g_words%d" % h, align_bytes=64)
+            nc.vector.tensor_copy(words[:], x_words[:].indirect(offsets[:, columns]))
+            if h == 1:
+                prepare_w("A01", 0, block0, (0, 1))
+            scales = keep.tile([P, 2 * V], U8, name="g_bytes%d" % h, tag=("g_bytes0", "w_grouped_A01")[h], align_bytes=64)
+            nc.vector.tensor_copy(scales[:], x_bytes[:].indirect(offsets[:, columns]))
+            g_words.append(words)
+            g_bytes.append(scales)
+
+        prepare_w("A2", 0, block0, (2,))
+        prepare_w("A3", 0, block0, (3,))
+        prepare_w("B", 0, block1, (0, 1, 2, 3))
 
         product(0)
+        y0 = activate(0, (bias_of(0), bias_of(0)), "y0", "y0")
+        scatter(0, y0, 0, 1)
         product(1)
-        put_back(0, 0, 128, "y0a")
-        put_back(1, 0, 256, "y1a")
-        put_back(0, 128, 640, "y0b")
-        put_back(1, 256, 768, "y1b")
-        prepare_w("1_d01", 1, 0, 0, 2 * M, M)
-        put_back(0, 640, 1024, "w_raw10")
-        prepare_w("1_d23", 1, 1, 0, 2 * M, M)
-        put_back(1, 768, 1024, "w_raw11")
+        y1 = activate(1, (bias_block1[0][:], bias_block1[1][:]), "y1", "y1")
+        scatter(1, y1, 0, 2)
+        scatter(0, y0, 1, 2)
+
+        prepare_w("C0", 1, both_blocks, (0, 1))
+        prepare_w("C1", 1, both_blocks, (2, 3))
+        scatter(1, activate(1, (bias_of(1), bias_of(1)), "y1_last", "w_raw10"), 2, 2)
+        scatter(0, activate(0, (bias_of(0),), "y0_last", "w_raw11"), 3, 1)
+
         product(2)
         product(3)
-        for e in (0, 512):
+        for d0 in (0, 2):
             for m in (2, 3):
-                put_back(m, e, e + 512, "y%d_%d" % (m, e))
+                y = activate(m, (bias_of(m), bias_of(m)), "y%d_%d" % (m, d0), "y%d_%d" % (m, d0))
+                scatter(m, y, d0, 2)

from contextlib import ExitStack

import concourse.mybir as mybir
from concourse.masks import make_identity

F32 = mybir.dt.float32
BF16 = mybir.dt.bfloat16
U32 = mybir.dt.uint32
U16 = mybir.dt.uint16
U8 = mybir.dt.uint8
FP8X4 = mybir.dt.float8_e4m3fn_x4
MULT = mybir.AluOpType.mult
GELU = mybir.ActivationFunctionType.Gelu_apprx_tanh

P = 128
K, T, D, V, N = 512, 1024, 4, 256, 512
PACK = K // P
BLOCKS = N // P
HALF = 2 * P
OFFSETS = 16
FLOPS = 2 * D * K * N * V

TOKEN_CHUNKS = ((0, 384, 256), (384, 384, 256), (768, 256, 176))
QUANTISE_TOKENS = 256


def interleave(copy, grouped, raw):
    copy(
        grouped.rearrange("p (c i) j -> p c j i", i=4),
        raw.rearrange("p j (c i) -> p c j i", i=4),
    )


def quantise(nc, words, scales, grouped):
    nc.vector.quantize_mx(out=words.bitcast(FP8X4), scales=scales, in_=grouped.rearrange("p c j -> p (c j)"))


def tile_picked_tome_lin_gelu_sub_e_kernel(tc, xT, w, b, gate, offs, out):
    nc = tc.nc
    with ExitStack() as ctx:
        keep = ctx.enter_context(tc.tile_pool(name="keep", bufs=1))
        psum = ctx.enter_context(tc.psum_pool(name="psum", bufs=1))

        bias_rows = keep.tile([P, P], F32, name="bias_rows")
        nc.gpsimd.memset(bias_rows[:], 0.0)
        nc.scalar.dma_start(bias_rows[0:BLOCKS, :], b.rearrange("(m p) o -> m (p o)", p=P))
        identity = keep.tile([P, P], F32, name="identity")
        make_identity(nc, identity[:])
        bias_columns = psum.tile([P, P], F32, name="bias_columns")
        nc.tensor.transpose(bias_columns[:], bias_rows[:], identity[:])
        bias = keep.tile([P, BLOCKS], F32, name="bias")
        nc.scalar.copy(bias[:], bias_columns[:, 0:BLOCKS])
        bias_block1 = []
        for h in range(2):
            column = keep.tile([P, 1], F32, name="bias_block1_%d" % h, tag="w_grouped_C%d" % h, align_bytes=64)
            nc.scalar.copy(column[:], bias_columns[:, 1:2])
            bias_block1.append(column)

        warm = keep.tile([P, 1], F32, name="warm")
        nc.vector.memset(warm[:], 0.0)
        nc.scalar.activation(warm[:], warm[:], GELU)

        x_words = keep.tile([P, T], U32, name="x_words", align_bytes=64)
        x_bytes = keep.tile([P, T], U8, name="x_bytes", align_bytes=64)
        nc.gpsimd.memset(x_bytes[:], 0)

        offsets = keep.tile([P, T // OFFSETS], U16, name="offsets")
        x_raw = []
        for i, (t0, n, _) in enumerate(TOKEN_CHUNKS):
            raw = keep.tile([P, PACK, n], F32, name="x_raw%d" % i)
            nc.sync.dma_start(raw[:], xT[:, t0 : t0 + n].rearrange("(p j) t -> p j t", j=PACK))
            x_raw.append(raw)
            if i == 1:
                nc.sync.dma_start(offsets[:], offs)

        w_raw = [
            [keep.tile([P, PACK, 2 * HALF], F32, name="w_raw%d%d" % (q, h), tag="w_raw%d%d" % (q, h)) for h in range(2)]
            for q in range(2)
        ]
        gates = [keep.tile([P, T], F32, name="gate%d" % m) for m in range(BLOCKS)]
        for q in range(2):
            for d in range(D):
                nc.sync.dma_start(
                    w_raw[q][d // 2][:, :, d % 2 * HALF : (d % 2 + 1) * HALF],
                    w[d, :, q * HALF : (q + 1) * HALF].rearrange("(p j) r -> p j r", j=PACK),
                )
            for m in (2 * q, 2 * q + 1):
                nc.sync.dma_start(gates[m][:], gate[m * P : (m + 1) * P, :])

        for i, (t0, n, h) in enumerate(TOKEN_CHUNKS):
            grouped = keep.tile([P, n, PACK], BF16, name="x_grouped%d" % i, align_bytes=64)
            interleave(nc.vector.tensor_copy, grouped[:, 0:h, :], x_raw[i][:, :, 0:h])
            interleave(nc.scalar.copy, grouped[:, h:n, :], x_raw[i][:, :, h:n])
            for q0 in range(0, n, QUANTISE_TOKENS):
                q1 = min(n, q0 + QUANTISE_TOKENS)
                tokens = slice(t0 + q0, t0 + q1)
                quantise(nc, x_words[:, tokens], x_bytes[:, tokens], grouped[:, q0:q1, :])

        w_codes = {}

        def prepare_w(name, q, rows, places):
            count = len(rows)
            width = count * len(places)
            grouped = keep.tile([P, width, PACK], BF16, name="w_grouped_" + name, tag="w_grouped_" + name, align_bytes=64)
            words = keep.tile([P, width], U32, name="w_words_" + name, align_bytes=64)
            scales = keep.tile([P, width], U8, name="w_bytes_" + name, align_bytes=64)
            for i, d in enumerate(places):
                c0 = d % 2 * HALF + rows[0]
                interleave(
                    nc.scalar.copy,
                    grouped[:, i * count : (i + 1) * count, :],
                    w_raw[q][d // 2][:, :, c0 : c0 + count],
                )
                for r in range(0, count, P):
                    cols = slice(i * count + r, i * count + r + P)
                    w_codes[(q * HALF + rows[0] + r) // P, d] = (words[:, cols], scales[:, cols])
            quantise(nc, words[:], scales[:], grouped[:])

        accs = [psum.tile([P, V], F32, name="acc%d" % m) for m in range(BLOCKS)]
        windows = [keep.tile([P, T], F32, name="window%d" % m) for m in range(BLOCKS)]
        g_words, g_bytes = [], []

        def product(m):
            for d in range(D):
                words, scales = w_codes[m, d]
                piece = slice(d % 2 * V, (d % 2 + 1) * V)
                nc.tensor.matmul_mx(
                    out=accs[m][:],
                    lhsT=words.bitcast(FP8X4),
                    lhsT_scale=scales,
                    rhs=g_words[d // 2][:, piece].bitcast(FP8X4),
                    rhs_scale=g_bytes[d // 2][:, piece],
                    start=(d == 0),
                    stop=(d == D - 1),
                )

        def activate(m, columns, name, tag):
            y = keep.tile([P, len(columns) * V], F32, name=name, tag=tag)
            for r, column in enumerate(columns):
                nc.scalar.activation(y[:, r * V : (r + 1) * V], accs[m][:], GELU, bias=column)
            return y

        def scatter(m, y, d0, count):
            entries = slice(d0 * V, (d0 + count) * V)
            nc.vector.tensor_tensor(
                windows[m][:].indirect(offsets[:, d0 * V // OFFSETS : (d0 + count) * V // OFFSETS]),
                y[:, 0 : count * V],
                gates[m][:, entries],
                MULT,
            )
            if d0 + count == D:
                nc.sync.dma_start(out[m * P : (m + 1) * P, :], windows[m][:])

        def bias_of(m):
            return bias[:, m : m + 1]

        block0, block1, both_blocks = range(0, P), range(P, HALF), range(0, HALF)

        for h in range(2):
            columns = slice(h * 2 * V // OFFSETS, (h + 1) * 2 * V // OFFSETS)
            words = keep.tile([P, 2 * V], U32, name="g_words%d" % h, align_bytes=64)
            nc.vector.tensor_copy(words[:], x_words[:].indirect(offsets[:, columns]))
            if h == 1:
                prepare_w("A01", 0, block0, (0, 1))
            scales = keep.tile([P, 2 * V], U8, name="g_bytes%d" % h, tag=("g_bytes0", "w_grouped_A01")[h], align_bytes=64)
            nc.vector.tensor_copy(scales[:], x_bytes[:].indirect(offsets[:, columns]))
            g_words.append(words)
            g_bytes.append(scales)

        prepare_w("A2", 0, block0, (2,))
        prepare_w("A3", 0, block0, (3,))
        prepare_w("B", 0, block1, (0, 1, 2, 3))

        product(0)
        y0 = activate(0, (bias_of(0), bias_of(0)), "y0", "y0")
        scatter(0, y0, 0, 1)
        product(1)
        y1 = activate(1, (bias_block1[0][:], bias_block1[1][:]), "y1", "y1")
        scatter(1, y1, 0, 2)
        scatter(0, y0, 1, 2)

        prepare_w("C0", 1, both_blocks, (0, 1))
        prepare_w("C1", 1, both_blocks, (2, 3))
        scatter(1, activate(1, (bias_of(1), bias_of(1)), "y1_last", "w_raw10"), 2, 2)
        scatter(0, activate(0, (bias_of(0),), "y0_last", "w_raw11"), 3, 1)

        product(2)
        product(3)
        for d0 in (0, 2):
            for m in (2, 3):
                y = activate(m, (bias_of(m), bias_of(m)), "y%d_%d" % (m, d0), "y%d_%d" % (m, d0))
                scatter(m, y, d0, 2)
